import numpy as np
import ml_dtypes

BF16 = ml_dtypes.bfloat16


def bf(x):
    return np.asarray(x, np.float32).astype(BF16)


def f32(x):
    return np.asarray(x, np.float32)


def f64(x):
    return np.asarray(x).astype(np.float64)


def striped(idx):
    return np.tile(idx.reshape(-1, 16).T, (8, 1))


S, K, M, N, E, Q = 512, 128, 128, 256, 4, 64


def setup_inputs():
    return {"base": bf(np.random.standard_normal((M, S))), "x": bf(np.random.standard_normal((K, N))), "w": bf(np.random.standard_normal((E, K, M)) / np.sqrt(K)), "b": f32(0.5 * np.random.standard_normal((M, 1))), "offs": striped(np.random.permutation(S)[:N])}


def reference(base, x, w, b, offs):
    idx = offs[:16].T.reshape(-1)
    z = f64(base).copy()
    for e in range(E):
        z[:, idx[e * Q : (e + 1) * Q]] += f64(w)[e].T @ f64(x)[:, e * Q : (e + 1) * Q]
    return np.tanh(z + f64(b))

@@ -1,0 +1,52 @@
+import concourse.mybir as mybir
+from concourse.masks import make_identity
+
+BF16, F32, U16 = mybir.dt.bfloat16, mybir.dt.float32, mybir.dt.uint16
+TANH = mybir.ActivationFunctionType.Tanh
+
+P = 128
+TOKENS = 512
+ENTRIES = 256
+EXPERTS = 4
+PIECE = ENTRIES // EXPERTS
+PIECE_COLS = PIECE // 16
+
+FLOPS = 2 * P * P * ENTRIES
+
+
+def tile_scatter_matmul_kernel(tc, base, x, w, b, offs, out):
+    nc = tc.nc
+    with (
+        tc.tile_pool(name="held", bufs=1) as held,
+        tc.psum_pool(name="psum", bufs=1) as psum,
+    ):
+        offsets = held.tile([P, ENTRIES // 16], U16, name="offsets")
+        nc.sync.dma_start(offsets[:], offs)
+
+        base_tile = held.tile([P, TOKENS], BF16, name="base_tile")
+        nc.scalar.dma_start(base_tile[:], base)
+        x_tile = held.tile([P, ENTRIES], BF16, name="x_tile")
+        nc.sync.dma_start(x_tile[:], x)
+        w_tile = held.tile([P, EXPERTS, P], BF16, name="w_tile")
+        nc.sync.dma_start(w_tile[:], w.rearrange("e k m -> k e m"))
+        bias = held.tile([P, 1], F32, name="bias")
+        nc.scalar.dma_start(bias[:], b)
+
+        ident = held.tile([P, P], BF16, name="ident")
+        make_identity(nc, ident[:])
+
+        window = psum.tile([P, TOKENS], F32, name="window")
+        nc.tensor.matmul(window[:], ident[:], base_tile[:], start=True, stop=False)
+
+        for e in range(EXPERTS):
+            nc.tensor.matmul(
+                window[:].indirect(offsets[:, e * PIECE_COLS : (e + 1) * PIECE_COLS]),
+                w_tile[:, e, :],
+                x_tile[:, e * PIECE : (e + 1) * PIECE],
+                start=False,
+                stop=(e == EXPERTS - 1),
+            )
+
+        result = held.tile([P, TOKENS], F32, name="result")
+        nc.scalar.activation(result[:], window[:], TANH, bias=bias[:])
+        nc.sync.dma_start(out, result[:])

@@ -35,6 +35,10 @@ def tile_scatter_matmul_kernel(tc, base, x, w, b, offs, out):
         ident = held.tile([P, P], BF16, name="ident")
         make_identity(nc, ident[:])
 
+        warm = held.tile([P, 1], F32, name="warm")
+        nc.vector.memset(warm[:], 0.0)
+        nc.scalar.activation(warm[:], warm[:], TANH)
+
         window = psum.tile([P, TOKENS], F32, name="window")
         nc.tensor.matmul(window[:], ident[:], base_tile[:], start=True, stop=False)
 

@@ -10,6 +10,8 @@ ENTRIES = 256
 EXPERTS = 4
 PIECE = ENTRIES // EXPERTS
 PIECE_COLS = PIECE // 16
+PARTS = 2
+PART_COLS = TOKENS // PARTS
 
 FLOPS = 2 * P * P * ENTRIES
 
@@ -52,5 +54,8 @@ def tile_scatter_matmul_kernel(tc, base, x, w, b, offs, out):
             )
 
         result = held.tile([P, TOKENS], F32, name="result")
-        nc.scalar.activation(result[:], window[:], TANH, bias=bias[:])
-        nc.sync.dma_start(out, result[:])
+        for part in range(PARTS):
+            cols = slice(part * PART_COLS, (part + 1) * PART_COLS)
+            nc.scalar.activation(result[:, cols], window[:, cols], TANH, bias=bias[:])
+            queue = nc.scalar if part % 2 == 1 else nc.sync
+            queue.dma_start(out[:, cols], result[:, cols])

@@ -10,8 +10,7 @@ ENTRIES = 256
 EXPERTS = 4
 PIECE = ENTRIES // EXPERTS
 PIECE_COLS = PIECE // 16
-PARTS = 2
-PART_COLS = TOKENS // PARTS
+WAKING_MATMULS = 2048 // TOKENS
 
 FLOPS = 2 * P * P * ENTRIES
 
@@ -41,6 +40,12 @@ def tile_scatter_matmul_kernel(tc, base, x, w, b, offs, out):
         nc.vector.memset(warm[:], 0.0)
         nc.scalar.activation(warm[:], warm[:], TANH)
 
+        zeros = held.tile([P, TOKENS], BF16, name="zeros")
+        nc.vector.memset(zeros[:], 0.0)
+        unread = psum.tile([P, TOKENS], F32, name="unread")
+        for _ in range(WAKING_MATMULS):
+            nc.tensor.matmul(unread[:], zeros[:, :P], zeros[:], start=True, stop=True)
+
         window = psum.tile([P, TOKENS], F32, name="window")
         nc.tensor.matmul(window[:], ident[:], base_tile[:], start=True, stop=False)
 
@@ -54,8 +59,5 @@ def tile_scatter_matmul_kernel(tc, base, x, w, b, offs, out):
             )
 
         result = held.tile([P, TOKENS], F32, name="result")
-        for part in range(PARTS):
-            cols = slice(part * PART_COLS, (part + 1) * PART_COLS)
-            nc.scalar.activation(result[:, cols], window[:, cols], TANH, bias=bias[:])
-            queue = nc.scalar if part % 2 == 1 else nc.sync
-            queue.dma_start(out[:, cols], result[:, cols])
+        nc.scalar.activation(result[:], window[:], TANH, bias=bias[:])
+        nc.sync.dma_start(out, result[:])

@@ -36,15 +36,15 @@ def tile_scatter_matmul_kernel(tc, base, x, w, b, offs, out):
         ident = held.tile([P, P], BF16, name="ident")
         make_identity(nc, ident[:])
 
-        warm = held.tile([P, 1], F32, name="warm")
-        nc.vector.memset(warm[:], 0.0)
-        nc.scalar.activation(warm[:], warm[:], TANH)
-
         zeros = held.tile([P, TOKENS], BF16, name="zeros")
-        nc.vector.memset(zeros[:], 0.0)
+        nc.vector.memset(zeros[:].bitcast(F32), 0.0)
         unread = psum.tile([P, TOKENS], F32, name="unread")
         for _ in range(WAKING_MATMULS):
             nc.tensor.matmul(unread[:], zeros[:, :P], zeros[:], start=True, stop=True)
+
+        warm = held.tile([P, 1], F32, name="warm")
+        nc.vector.memset(warm[:], 0.0)
+        nc.scalar.activation(warm[:], warm[:], TANH)
 
         window = psum.tile([P, TOKENS], F32, name="window")
         nc.tensor.matmul(window[:], ident[:], base_tile[:], start=True, stop=False)

@@ -21,17 +21,18 @@ def tile_scatter_matmul_kernel(tc, base, x, w, b, offs, out):
         tc.tile_pool(name="held", bufs=1) as held,
         tc.psum_pool(name="psum", bufs=1) as psum,
     ):
+        base_tile = held.tile([P, TOKENS], BF16, name="base_tile")
+        nc.sync.dma_start(base_tile[:], base)
+
         offsets = held.tile([P, ENTRIES // 16], U16, name="offsets")
         nc.sync.dma_start(offsets[:], offs)
 
-        base_tile = held.tile([P, TOKENS], BF16, name="base_tile")
-        nc.scalar.dma_start(base_tile[:], base)
         x_tile = held.tile([P, ENTRIES], BF16, name="x_tile")
         nc.sync.dma_start(x_tile[:], x)
         w_tile = held.tile([P, EXPERTS, P], BF16, name="w_tile")
         nc.sync.dma_start(w_tile[:], w.rearrange("e k m -> k e m"))
         bias = held.tile([P, 1], F32, name="bias")
-        nc.scalar.dma_start(bias[:], b)
+        nc.sync.dma_start(bias[:], b)
 
         ident = held.tile([P, P], BF16, name="ident")
         make_identity(nc, ident[:])

@@ -37,11 +37,12 @@ def tile_scatter_matmul_kernel(tc, base, x, w, b, offs, out):
         ident = held.tile([P, P], BF16, name="ident")
         make_identity(nc, ident[:])
 
-        zeros = held.tile([P, TOKENS], BF16, name="zeros")
+        zeros = held.tile([P, P], BF16, name="zeros")
         nc.vector.memset(zeros[:].bitcast(F32), 0.0)
+        zeros_repeated = zeros[:].unsqueeze(1).to_broadcast([P, TOKENS // P, P])
         unread = psum.tile([P, TOKENS], F32, name="unread")
         for _ in range(WAKING_MATMULS):
-            nc.tensor.matmul(unread[:], zeros[:, :P], zeros[:], start=True, stop=True)
+            nc.tensor.matmul(unread[:], zeros[:], zeros_repeated, start=True, stop=True)
 
         warm = held.tile([P, 1], F32, name="warm")
         nc.vector.memset(warm[:], 0.0)

@@ -10,7 +10,7 @@ ENTRIES = 256
 EXPERTS = 4
 PIECE = ENTRIES // EXPERTS
 PIECE_COLS = PIECE // 16
-WAKING_MATMULS = 2048 // TOKENS
+WAKING_MATMULS = 1024 // TOKENS
 
 FLOPS = 2 * P * P * ENTRIES
 

@@ -10,6 +10,7 @@ ENTRIES = 256
 EXPERTS = 4
 PIECE = ENTRIES // EXPERTS
 PIECE_COLS = PIECE // 16
+BLOCK = 32
 WAKING_MATMULS = 1024 // TOKENS
 
 FLOPS = 2 * P * P * ENTRIES
@@ -31,8 +32,6 @@ def tile_scatter_matmul_kernel(tc, base, x, w, b, offs, out):
         nc.sync.dma_start(x_tile[:], x)
         w_tile = held.tile([P, EXPERTS, P], BF16, name="w_tile")
         nc.sync.dma_start(w_tile[:], w.rearrange("e k m -> k e m"))
-        bias = held.tile([P, 1], F32, name="bias")
-        nc.sync.dma_start(bias[:], b)
 
         ident = held.tile([P, P], BF16, name="ident")
         make_identity(nc, ident[:])
@@ -43,6 +42,13 @@ def tile_scatter_matmul_kernel(tc, base, x, w, b, offs, out):
         unread = psum.tile([P, TOKENS], F32, name="unread")
         for _ in range(WAKING_MATMULS):
             nc.tensor.matmul(unread[:], zeros[:], zeros_repeated, start=True, stop=True)
+
+        bias_rows = held.tile([P, BLOCK], F32, name="bias_rows", align_bytes=64)
+        nc.vector.memset(bias_rows[:], 0.0)
+        nc.scalar.dma_start(bias_rows[::BLOCK, :], b.rearrange("(q j) o -> q (j o)", j=BLOCK))
+        bias_columns = held.tile([P, BLOCK], F32, name="bias_columns", align_bytes=64)
+        nc.vector.transpose(bias_columns[:], bias_rows[:])
+        bias = bias_columns[:, 0:1]
 
         warm = held.tile([P, 1], F32, name="warm")
         nc.vector.memset(warm[:], 0.0)
@@ -61,5 +67,5 @@ def tile_scatter_matmul_kernel(tc, base, x, w, b, offs, out):
             )
 
         result = held.tile([P, TOKENS], F32, name="result")
-        nc.scalar.activation(result[:], window[:], TANH, bias=bias[:])
+        nc.scalar.activation(result[:], window[:], TANH, bias=bias)
         nc.sync.dma_start(out, result[:])

@@ -10,6 +10,7 @@ ENTRIES = 256
 EXPERTS = 4
 PIECE = ENTRIES // EXPERTS
 PIECE_COLS = PIECE // 16
+PER_LOAD = 2
 BLOCK = 32
 WAKING_MATMULS = 1024 // TOKENS
 
@@ -30,8 +31,12 @@ def tile_scatter_matmul_kernel(tc, base, x, w, b, offs, out):
 
         x_tile = held.tile([P, ENTRIES], BF16, name="x_tile")
         nc.sync.dma_start(x_tile[:], x)
-        w_tile = held.tile([P, EXPERTS, P], BF16, name="w_tile")
-        nc.sync.dma_start(w_tile[:], w.rearrange("e k m -> k e m"))
+        w_tiles = []
+        for h in range(EXPERTS // PER_LOAD):
+            w_tiles.append(held.tile([P, PER_LOAD, P], BF16, name="w_tile%d" % h))
+            nc.sync.dma_start(
+                w_tiles[h][:], w[h * PER_LOAD : (h + 1) * PER_LOAD].rearrange("e k m -> k e m")
+            )
 
         ident = held.tile([P, P], BF16, name="ident")
         make_identity(nc, ident[:])
@@ -60,7 +65,7 @@ def tile_scatter_matmul_kernel(tc, base, x, w, b, offs, out):
         for e in range(EXPERTS):
             nc.tensor.matmul(
                 window[:].indirect(offsets[:, e * PIECE_COLS : (e + 1) * PIECE_COLS]),
-                w_tile[:, e, :],
+                w_tiles[e // PER_LOAD][:, e % PER_LOAD, :],
                 x_tile[:, e * PIECE : (e + 1) * PIECE],
                 start=False,
                 stop=(e == EXPERTS - 1),

@@ -23,6 +23,11 @@ def tile_scatter_matmul_kernel(tc, base, x, w, b, offs, out):
         tc.tile_pool(name="held", bufs=1) as held,
         tc.psum_pool(name="psum", bufs=1) as psum,
     ):
+        bias_rows = held.tile([P, BLOCK], F32, name="bias_rows", align_bytes=64)
+        nc.scalar.dma_start(
+            bias_rows[BLOCK - 1 :: BLOCK, :], b.rearrange("(q j) o -> q (j o)", j=BLOCK)
+        )
+
         base_tile = held.tile([P, TOKENS], BF16, name="base_tile")
         nc.sync.dma_start(base_tile[:], base)
 
@@ -48,16 +53,15 @@ def tile_scatter_matmul_kernel(tc, base, x, w, b, offs, out):
         for _ in range(WAKING_MATMULS):
             nc.tensor.matmul(unread[:], zeros[:], zeros_repeated, start=True, stop=True)
 
-        bias_rows = held.tile([P, BLOCK], F32, name="bias_rows", align_bytes=64)
-        nc.vector.memset(bias_rows[:], 0.0)
-        nc.scalar.dma_start(bias_rows[::BLOCK, :], b.rearrange("(q j) o -> q (j o)", j=BLOCK))
-        bias_columns = held.tile([P, BLOCK], F32, name="bias_columns", align_bytes=64)
-        nc.vector.transpose(bias_columns[:], bias_rows[:])
-        bias = bias_columns[:, 0:1]
-
         warm = held.tile([P, 1], F32, name="warm")
         nc.vector.memset(warm[:], 0.0)
         nc.scalar.activation(warm[:], warm[:], TANH)
+
+        for q in range(P // BLOCK):
+            nc.vector.memset(bias_rows[q * BLOCK : (q + 1) * BLOCK - 1, :], 0.0)
+        bias_columns = held.tile([P, BLOCK], F32, name="bias_columns", align_bytes=64)
+        nc.vector.transpose(bias_columns[:], bias_rows[:])
+        bias = bias_columns[:, BLOCK - 1 : BLOCK]
 
         window = psum.tile([P, TOKENS], F32, name="window")
         nc.tensor.matmul(window[:], ident[:], base_tile[:], start=True, stop=False)

@@ -12,6 +12,7 @@ PIECE = ENTRIES // EXPERTS
 PIECE_COLS = PIECE // 16
 PER_LOAD = 2
 BLOCK = 32
+BUS_BYTES = 256
 WAKING_MATMULS = 1024 // TOKENS
 
 FLOPS = 2 * P * P * ENTRIES
@@ -28,17 +29,19 @@ def tile_scatter_matmul_kernel(tc, base, x, w, b, offs, out):
             bias_rows[BLOCK - 1 :: BLOCK, :], b.rearrange("(q j) o -> q (j o)", j=BLOCK)
         )
 
-        base_tile = held.tile([P, TOKENS], BF16, name="base_tile")
+        base_tile = held.tile([P, TOKENS], BF16, name="base_tile", align_bytes=BUS_BYTES)
         nc.sync.dma_start(base_tile[:], base)
 
         offsets = held.tile([P, ENTRIES // 16], U16, name="offsets")
         nc.sync.dma_start(offsets[:], offs)
 
-        x_tile = held.tile([P, ENTRIES], BF16, name="x_tile")
+        x_tile = held.tile([P, ENTRIES], BF16, name="x_tile", align_bytes=BUS_BYTES)
         nc.sync.dma_start(x_tile[:], x)
         w_tiles = []
         for h in range(EXPERTS // PER_LOAD):
-            w_tiles.append(held.tile([P, PER_LOAD, P], BF16, name="w_tile%d" % h))
+            w_tiles.append(
+                held.tile([P, PER_LOAD, P], BF16, name="w_tile%d" % h, align_bytes=BUS_BYTES)
+            )
             nc.sync.dma_start(
                 w_tiles[h][:], w[h * PER_LOAD : (h + 1) * PER_LOAD].rearrange("e k m -> k e m")
             )
@@ -75,6 +78,6 @@ def tile_scatter_matmul_kernel(tc, base, x, w, b, offs, out):
                 stop=(e == EXPERTS - 1),
             )
 
-        result = held.tile([P, TOKENS], F32, name="result")
+        result = held.tile([P, TOKENS], F32, name="result", align_bytes=BUS_BYTES)
         nc.scalar.activation(result[:], window[:], TANH, bias=bias)
         nc.sync.dma_start(out, result[:])

@@ -46,11 +46,12 @@ def tile_scatter_matmul_kernel(tc, base, x, w, b, offs, out):
                 w_tiles[h][:], w[h * PER_LOAD : (h + 1) * PER_LOAD].rearrange("e k m -> k e m")
             )
 
+        zeros = held.tile([P, P], BF16, name="zeros")
+        nc.gpsimd.memset(zeros[:].bitcast(F32), 0.0)
+
         ident = held.tile([P, P], BF16, name="ident")
         make_identity(nc, ident[:])
 
-        zeros = held.tile([P, P], BF16, name="zeros")
-        nc.vector.memset(zeros[:].bitcast(F32), 0.0)
         zeros_repeated = zeros[:].unsqueeze(1).to_broadcast([P, TOKENS // P, P])
         unread = psum.tile([P, TOKENS], F32, name="unread")
         for _ in range(WAKING_MATMULS):

import concourse.mybir as mybir
from concourse.masks import make_identity

BF16, F32, U16 = mybir.dt.bfloat16, mybir.dt.float32, mybir.dt.uint16
TANH = mybir.ActivationFunctionType.Tanh

P = 128
TOKENS = 512
ENTRIES = 256
EXPERTS = 4
PIECE = ENTRIES // EXPERTS
PIECE_COLS = PIECE // 16
PER_LOAD = 2
BLOCK = 32
BUS_BYTES = 256
WAKING_MATMULS = 1024 // TOKENS

FLOPS = 2 * P * P * ENTRIES


def tile_scatter_matmul_kernel(tc, base, x, w, b, offs, out):
    nc = tc.nc
    with (
        tc.tile_pool(name="held", bufs=1) as held,
        tc.psum_pool(name="psum", bufs=1) as psum,
    ):
        bias_rows = held.tile([P, BLOCK], F32, name="bias_rows", align_bytes=64)
        nc.scalar.dma_start(
            bias_rows[BLOCK - 1 :: BLOCK, :], b.rearrange("(q j) o -> q (j o)", j=BLOCK)
        )

        base_tile = held.tile([P, TOKENS], BF16, name="base_tile", align_bytes=BUS_BYTES)
        nc.sync.dma_start(base_tile[:], base)

        offsets = held.tile([P, ENTRIES // 16], U16, name="offsets")
        nc.sync.dma_start(offsets[:], offs)

        x_tile = held.tile([P, ENTRIES], BF16, name="x_tile", align_bytes=BUS_BYTES)
        nc.sync.dma_start(x_tile[:], x)
        w_tiles = []
        for h in range(EXPERTS // PER_LOAD):
            w_tiles.append(
                held.tile([P, PER_LOAD, P], BF16, name="w_tile%d" % h, align_bytes=BUS_BYTES)
            )
            nc.sync.dma_start(
                w_tiles[h][:], w[h * PER_LOAD : (h + 1) * PER_LOAD].rearrange("e k m -> k e m")
            )

        zeros = held.tile([P, P], BF16, name="zeros")
        nc.gpsimd.memset(zeros[:].bitcast(F32), 0.0)

        ident = held.tile([P, P], BF16, name="ident")
        make_identity(nc, ident[:])

        zeros_repeated = zeros[:].unsqueeze(1).to_broadcast([P, TOKENS // P, P])
        unread = psum.tile([P, TOKENS], F32, name="unread")
        for _ in range(WAKING_MATMULS):
            nc.tensor.matmul(unread[:], zeros[:], zeros_repeated, start=True, stop=True)

        warm = held.tile([P, 1], F32, name="warm")
        nc.vector.memset(warm[:], 0.0)
        nc.scalar.activation(warm[:], warm[:], TANH)

        for q in range(P // BLOCK):
            nc.vector.memset(bias_rows[q * BLOCK : (q + 1) * BLOCK - 1, :], 0.0)
        bias_columns = held.tile([P, BLOCK], F32, name="bias_columns", align_bytes=64)
        nc.vector.transpose(bias_columns[:], bias_rows[:])
        bias = bias_columns[:, BLOCK - 1 : BLOCK]

        window = psum.tile([P, TOKENS], F32, name="window")
        nc.tensor.matmul(window[:], ident[:], base_tile[:], start=True, stop=False)

        for e in range(EXPERTS):
            nc.tensor.matmul(
                window[:].indirect(offsets[:, e * PIECE_COLS : (e + 1) * PIECE_COLS]),
                w_tiles[e // PER_LOAD][:, e % PER_LOAD, :],
                x_tile[:, e * PIECE : (e + 1) * PIECE],
                start=False,
                stop=(e == EXPERTS - 1),
            )

        result = held.tile([P, TOKENS], F32, name="result", align_bytes=BUS_BYTES)
        nc.scalar.activation(result[:], window[:], TANH, bias=bias)
        nc.sync.dma_start(out, result[:])
